import numpy as np
import ml_dtypes


def mxq(x, axis, fmt="e4m3"):
    dtype, down = {"e4m3": (ml_dtypes.float8_e4m3fn, 7), "e5m2": (ml_dtypes.float8_e5m2, 14)}[fmt]
    v = np.moveaxis(np.asarray(x, np.float32).astype(ml_dtypes.bfloat16).astype(np.float64), axis, -1)
    blocks = v.reshape(v.shape[:-1] + (-1, 32))
    amax = np.abs(blocks).max(-1, keepdims=True)
    byte = np.maximum(np.where(amax > 0, np.frexp(amax)[1] - 1 + 127, 0) - down, 1)
    scale = np.exp2(byte - 127.0)
    codes = (blocks / scale).astype(np.float32).astype(dtype).astype(np.float64)
    return np.moveaxis((codes * scale).reshape(v.shape), -1, axis)


WIDE = False


def mx_kscale(k):
    if not WIDE:
        return np.ones(k)
    levels = np.array([10, -10, 5, -5, 0])
    if k % 512:
        return np.exp2(np.random.permutation(np.resize(levels, k // 32))).repeat(32)
    a = np.empty((k // 512, 16))
    for p in range(k // 512):
        a[p, :8] = np.random.permutation(np.resize(levels, 8))
        for g in range(8):
            far = levels[np.abs(levels - a[p, g]) >= 10]
            a[p, g + 8] = far[np.random.randint(len(far))]
    return np.exp2(a.ravel()).repeat(32)


def f64(x):
    return np.asarray(x).astype(np.float64)


def striped(idx):
    return np.tile(idx.reshape(-1, 16).T, (8, 1)).astype(np.uint16)


def unstriped(offs):
    return offs[:16].T.reshape(-1).astype(np.int64)


def striped8(idx):
    return np.concatenate([x.reshape(-1, 16).T for x in idx]).astype(np.uint16)


def runs(offs, k):
    lists = np.stack([offs[16 * r : 16 * r + 16].T.reshape(-1) for r in range(8)]).astype(np.int64)
    return lists[np.arange(k) % 512 // 64]


def pack_weight(w):
    k, n = w.shape
    w = f64(np.asarray(w, np.float32).astype(ml_dtypes.bfloat16)).reshape(k // 32, 32, n)
    amax = np.abs(w).max(1)
    byte = np.clip(np.where(amax > 0, np.frexp(amax)[1] - 1 + 127 - 7, 1), 1, 254)
    scaled = (w * np.exp2(127.0 - byte)[:, None, :]).reshape(k, n).astype(np.float32)
    words = np.ascontiguousarray(scaled.reshape(k // 512, 128, 4, n).transpose(0, 1, 3, 2)).astype(ml_dtypes.float8_e4m3fn).view(np.uint8)
    return words, np.ascontiguousarray(byte.astype(np.uint8).reshape(k // 512, 16, n))


def unpack_weight(words, scales):
    g, p, n, _ = words.shape
    vals = np.ascontiguousarray(words).view(ml_dtypes.float8_e4m3fn).astype(np.float64) * np.repeat(np.exp2(scales.astype(np.float64) - 127.0), 8, axis=1)[..., None]
    return vals.transpose(0, 1, 3, 2).reshape(g * 512, n)

def planes(y):
    n, m = y.shape
    v = y.astype(np.float32).astype(ml_dtypes.bfloat16).astype(np.float64).reshape(n // 32, 32, m)
    top = np.abs(v).max(1)
    byte = np.clip(np.where(top > 0, np.frexp(top)[1] - 1 + 127 - 7, 1), 1, 254)
    codes = (v * np.exp2(127.0 - byte)[:, None, :]).reshape(n, m).astype(np.float32).astype(ml_dtypes.float8_e4m3fn).view(np.uint8)
    words = codes.reshape(n // 512, 128, 4, m).transpose(0, 1, 3, 2)
    return np.ascontiguousarray(words), np.ascontiguousarray(byte.astype(np.uint8).reshape(n // 512, 16, m))


K, T, S, H, C = 512, 2048, 512, 512, 512


def setup_inputs():
    n = np.random.standard_normal
    s = mx_kscale(K)[:, None]
    packed_xT = pack_weight(n((K, T)) * s)
    packed_w1 = pack_weight(n((K, H)) / np.sqrt(K) / s)
    return {
        "x_words": packed_xT[0],
        "x_scales": packed_xT[1],
        "w1_words": packed_w1[0],
        "w1_scales": packed_w1[1],
        "gs": (np.random.uniform(0.5, 1.5, (K, 1)) / s).astype(np.float32),
        "offs": striped(np.random.permutation(T)[:S]),
        "n1": striped8(np.stack([np.random.permutation(S) for _ in range(8)])),
        "n2": striped8(np.stack([np.random.permutation(S) for _ in range(8)])),
        "n3": striped8(np.stack([np.random.permutation(S) for _ in range(8)])),
        "ca": striped(np.random.permutation(T)[:C]),
        "cb": striped(np.random.permutation(T)[:C]),
        "n4": striped8(np.stack([np.random.permutation(S) for _ in range(8)])),
        "n5": striped8(np.stack([np.random.permutation(S) for _ in range(8)])),
        "n6": striped8(np.stack([np.random.permutation(S) for _ in range(8)])),
    }


def reference(x_words, x_scales, w1_words, w1_scales, gs, offs, n1, n2, n3, ca, cb, n4, n5, n6):
    x_ca = unpack_weight(x_words, x_scales)[:, unstriped(ca)]
    xq = unpack_weight(x_words, x_scales)[:, unstriped(offs)]
    y = unpack_weight(w1_words, w1_scales).T @ xq
    z = f64(gs) * (y + y[np.arange(H)[:, None], runs(n1, H)] - (np.maximum(y[np.arange(H)[:, None], runs(n2, H)], y[np.arange(H)[:, None], runs(n3, H)])))
    zq = mxq(z, 0, "e4m3")
    a = 0.0625 * (x_ca.T @ zq)
    x_cb = unpack_weight(x_words, x_scales)[:, unstriped(cb)]
    b = 0.0625 * (x_cb.T @ zq)
    out_0 = np.maximum(np.minimum(a - (0.5 * (a[np.arange(C)[:, None], runs(n4, C)])), b[np.arange(C)[:, None], runs(n5, C)]), b[np.arange(C)[:, None], runs(n6, C)])
    return (out_0,) + planes(out_0)

@@ -1,0 +1,214 @@
+from contextlib import ExitStack
+
+import concourse.mybir as mybir
+
+F32 = mybir.dt.float32
+BF16 = mybir.dt.bfloat16
+I32 = mybir.dt.int32
+U32 = mybir.dt.uint32
+U16 = mybir.dt.uint16
+U8 = mybir.dt.uint8
+FP8X4 = mybir.dt.float8_e4m3fn_x4
+ALU = mybir.AluOpType
+COPY = mybir.ActivationFunctionType.Copy
+
+P = 128
+PACK = 4
+T = 2048
+S = 512
+HALF = S // 2
+FLOPS = 3 * 2 * 512 * 512 * 512
+
+
+def tile_picked_ccmpclampbtrim_none_po_kernel(
+    tc, x_words, x_scales, w1_words, w1_scales, gs, offs, n1, n2, n3, ca, cb, n4, n5, n6, out_0, out_1, out_2
+):
+    nc = tc.nc
+    with ExitStack() as ctx:
+        keep = ctx.enter_context(tc.tile_pool(name="keep", bufs=1))
+        ring = ctx.enter_context(tc.tile_pool(name="ring", bufs=2))
+        psum = ctx.enter_context(tc.psum_pool(name="psum", bufs=8))
+
+        def load_list(name, src):
+            tile = keep.tile([P, S // 16], U16, name=name)
+            nc.sync.dma_start(tile[:], src)
+            return tile
+
+        def load_scale_rows(tile, src):
+            for q in range(4):
+                nc.sync.dma_start(tile[32 * q : 32 * q + 4, :].bitcast(I32), src[0, 4 * q : 4 * q + 4, :].bitcast(I32))
+
+        def cols(h):
+            return slice(h * HALF, (h + 1) * HALF)
+
+        def entries(lst, h):
+            return lst[:, h * HALF // 16 : (h + 1) * HALF // 16]
+
+        def weave(engine_copy, dst, src):
+            engine_copy(
+                dst.rearrange("p (c i t) -> p c t i", i=4, t=PACK),
+                src.rearrange("p t (c i) -> p c t i", i=4),
+            )
+
+        def product(lhs_w, lhs_s, t, rhs_w, rhs_s, span):
+            width = span.stop - span.start
+            bank = psum.tile([P, width], F32, name="bank")
+            m = slice(t * P, (t + 1) * P)
+            nc.tensor.matmul_mx(
+                out=bank[:],
+                lhsT=lhs_w[:, m].bitcast(FP8X4),
+                lhsT_scale=lhs_s[:, m],
+                rhs=rhs_w[:, span].bitcast(FP8X4),
+                rhs_scale=rhs_s[:, span],
+                start=True,
+                stop=True,
+            )
+            return bank
+
+        x_s = keep.tile([P, T], U8, name="x_s", align_bytes=64)
+        x_w = keep.tile([P, T], U32, name="x_w", align_bytes=64)
+        w_s_raw = keep.tile([P, S], U8, name="w_s_raw", align_bytes=64)
+        w_w_raw = keep.tile([P, S], U32, name="w_w_raw", align_bytes=64)
+        nc.vector.memset(x_s[:].bitcast(I32), 0)
+        nc.vector.memset(w_s_raw[:].bitcast(I32), 0)
+
+        l_offs = load_list("l_offs", offs)
+        load_scale_rows(x_s, x_scales)
+        l_ca = load_list("l_ca", ca)
+        nc.sync.dma_start(w_w_raw[:].bitcast(I32), w1_words[0].rearrange("p n t -> p (n t)").bitcast(I32))
+        nc.sync.dma_start(x_w[:].bitcast(I32), x_words[0].rearrange("p n t -> p (n t)").bitcast(I32))
+        load_scale_rows(w_s_raw, w1_scales)
+        gain = keep.tile([P, PACK], F32, name="gain")
+        nc.sync.dma_start(gain[:], gs.rearrange("(p t) o -> p (t o)", t=PACK))
+        l_n2 = load_list("l_n2", n2)
+        l_n3 = load_list("l_n3", n3)
+        l_n1 = load_list("l_n1", n1)
+        l_cb = load_list("l_cb", cb)
+        l_n4 = load_list("l_n4", n4)
+        l_n5 = load_list("l_n5", n5)
+        l_n6 = load_list("l_n6", n6)
+
+        win_a = [keep.tile([P, 2 * S], F32, name=f"win_a{t}") for t in range(PACK)]
+        win_b = [keep.tile([P, 2 * S], F32, name=f"win_b{t}") for t in range(PACK)]
+        for t in range(PACK):
+            nc.gpsimd.memset(win_a[t][:, S:], 0.0)
+
+        neg_gain = keep.tile([P, PACK], F32, name="neg_gain")
+        nc.scalar.activation(neg_gain[:], gain[:], COPY, scale=-1.0)
+
+        xq_s = keep.tile([P, S], U8, name="xq_s", align_bytes=64)
+        xq_w = keep.tile([P, S], U32, name="xq_w", align_bytes=64)
+        nc.vector.tensor_copy(xq_s[:], x_s[:].indirect(l_offs[:]))
+        w_w = keep.tile([P, S], U32, name="w_w", align_bytes=64)
+        w_s = keep.tile([P, S], U8, name="w_s", align_bytes=64)
+        nc.vector.tensor_copy(
+            w_w[:].bitcast(I32).rearrange("p (t m) -> p t m", t=PACK),
+            w_w_raw[:].bitcast(I32).rearrange("p (m t) -> p t m", t=PACK),
+        )
+        nc.vector.tensor_copy(
+            w_s[:].rearrange("p (t m) -> p t m", t=PACK), w_s_raw[:].rearrange("p (m t) -> p t m", t=PACK)
+        )
+        for h in range(2):
+            nc.vector.tensor_copy(xq_w[:, cols(h)], x_w[:].indirect(entries(l_offs, h)))
+
+        def pick_scales(name, lst, tag):
+            listed = keep.tile([P, S], U8, name=name + "_listed", tag=tag, align_bytes=64)
+            nc.vector.tensor_copy(listed[:], x_s[:].indirect(lst[:]))
+            dealt = keep.tile([P, S], U8, name=name, align_bytes=64)
+            nc.vector.tensor_copy(
+                dealt[:].rearrange("p (t m) -> p t m", t=PACK), listed[:].rearrange("p (m t) -> p t m", t=PACK)
+            )
+            return dealt
+
+        def pick_words(name, lst, tag):
+            dealt = keep.tile([P, S], U32, name=name, tag=tag, align_bytes=64)
+            nc.vector.tensor_copy(dealt[:].rearrange("p (t m) -> p m t", t=PACK), x_w[:].indirect(lst[:]))
+            return dealt
+
+        ca_s = pick_scales("ca_s", l_ca, "ca_s_listed")
+        ca_w = pick_words("ca_w", l_ca, "w_s_raw")
+
+        spans = [[cols(0), cols(1)]] + [[slice(0, S)]] * (PACK - 1)
+        y_banks = []
+        for t in range(PACK):
+            for span in spans[t]:
+                bank = product(w_w, w_s, t, xq_w, xq_s, span)
+                nc.scalar.copy(win_a[t][:, span], bank[:])
+                nc.scalar.copy(win_b[t][:, S + span.start : S + span.stop], bank[:])
+                y_banks.append((t, span, bank))
+
+        rest = []
+        for t in range(PACK):
+            d2 = ring.tile([P, S], F32, name="d2")
+            d3 = ring.tile([P, S], F32, name="d3")
+            nc.vector.tensor_tensor(d2[:], win_a[t][:].indirect(l_n2[:]), win_b[t][:, S:], ALU.subtract)
+            nc.vector.tensor_tensor(d3[:], win_a[t][:].indirect(l_n3[:]), win_b[t][:, S:], ALU.subtract)
+            top = ring.tile([P, S], F32, name="top")
+            nc.vector.tensor_tensor(top[:], d2[:], d3[:], ALU.max)
+            r = keep.tile([P, S], F32, name=f"rest{t}", align_bytes=64)
+            nc.scalar.activation(r[:], top[:], COPY, scale=neg_gain[:, t : t + 1])
+            rest.append(r)
+            for tt, span, bank in y_banks:
+                if tt == t:
+                    nc.scalar.activation(win_b[t][:, span], bank[:], COPY, scale=gain[:, t : t + 1])
+
+        z_w = keep.tile([P, S], U32, name="z_w", align_bytes=64)
+        z_s = keep.tile([P, S], U8, name="z_s", align_bytes=64)
+        a_first = []
+        for h in range(2):
+            z = keep.tile([P, PACK, HALF], F32, name=f"z{h}")
+            for t in range(PACK):
+                nc.vector.tensor_tensor(z[:, t, :], win_b[t][:].indirect(entries(l_n1, h)), rest[t][:, cols(h)], ALU.add)
+            zb = keep.tile([P, PACK * HALF], BF16, name=f"zb{h}", align_bytes=64)
+            weave(nc.scalar.copy, zb[:], z[:])
+            nc.vector.quantize_mx(out=z_w[:, cols(h)].bitcast(FP8X4), scales=z_s[:, cols(h)], in_=zb[:])
+            a_first.append(product(ca_w, ca_s, 0, z_w, z_s, cols(h)))
+
+        cb_w = pick_words("cb_w", l_cb, f"rest{PACK - 1}")
+        cb_s = pick_scales("cb_s", l_cb, "zb1")
+
+        low = []
+        for t in range(PACK):
+            if t == 0:
+                a_banks = [(cols(h), a_first[h]) for h in range(2)]
+            else:
+                a_banks = [(slice(0, S), product(ca_w, ca_s, t, z_w, z_s, slice(0, S)))]
+            for span, bank in a_banks:
+                nc.scalar.activation(win_a[t][:, span], bank[:], COPY, scale=0.0625)
+                nc.scalar.activation(win_b[t][:, S + span.start : S + span.stop], bank[:], COPY, scale=0.125)
+            bank = product(cb_w, cb_s, t, z_w, z_s, slice(0, S))
+            nc.scalar.activation(win_b[t][:, :S], bank[:], COPY, scale=0.0625)
+            d4 = ring.tile([P, S], F32, name="d2")
+            g5 = ring.tile([P, S], F32, name="d3")
+            nc.vector.tensor_tensor(d4[:], win_a[t][:].indirect(l_n4[:]), win_b[t][:, S:], ALU.subtract)
+            nc.vector.tensor_copy(g5[:], win_b[t][:].indirect(l_n5[:]))
+            lo = keep.tile([P, S], F32, name=f"low{t}")
+            nc.vector.scalar_tensor_tensor(lo[:], d4[:], -0.5, g5[:], ALU.mult, ALU.min)
+            low.append(lo)
+
+        o_w = keep.tile([P, S], U32, name="o_w", align_bytes=64)
+        o_s = keep.tile([P, S], U8, name="o_s", align_bytes=64)
+        out_rows = out_0.rearrange("(p t) j -> p t j", t=PACK)
+        out_words = out_1[0].rearrange("p c r -> p (c r)").bitcast(I32)
+        for h in range(2):
+            o = keep.tile([P, PACK, HALF], F32, name=f"o{h}")
+            g6 = keep.tile([P, PACK, HALF], F32, name=f"g6{h}")
+            for t in range(PACK):
+                nc.vector.tensor_copy(g6[:, t, :], win_b[t][:].indirect(entries(l_n6, h)))
+                nc.vector.tensor_tensor(o[:, t, :], low[t][:, cols(h)], g6[:, t, :], ALU.max)
+            if h == 0:
+                nc.sync.dma_start(out_rows[:, :, cols(h)], o[:])
+                parts = [(nc.scalar.copy, 0, HALF)]
+            else:
+                nc.sync.dma_start(out_rows[:, 0:2, cols(h)], o[:, 0:2, :])
+                nc.sync.dma_start(out_rows[:, 2:4, cols(h)], o[:, 2:4, :])
+                parts = [(nc.vector.tensor_copy, 0, HALF // 2), (nc.scalar.copy, HALF // 2, HALF)]
+            for copy, c0, c1 in parts:
+                ob = keep.tile([P, PACK * (c1 - c0)], BF16, name=f"ob{h}_{c0}", align_bytes=64)
+                weave(copy, ob[:], o[:, :, c0:c1])
+                span = slice(h * HALF + c0, h * HALF + c1)
+                nc.vector.quantize_mx(out=o_w[:, span].bitcast(FP8X4), scales=o_s[:, span], in_=ob[:])
+            nc.sync.dma_start(out_words[:, cols(h)], o_w[:, cols(h)].bitcast(I32))
+        for q in range(4):
+            eng = nc.scalar if q % 2 == 0 else nc.sync
+            eng.dma_start(out_2[0, 4 * q : 4 * q + 4, :].bitcast(I32), o_s[32 * q : 32 * q + 4, :].bitcast(I32))

@@ -1,6 +1,7 @@
 from contextlib import ExitStack
 
 import concourse.mybir as mybir
+from concourse.masks import make_identity
 
 F32 = mybir.dt.float32
 BF16 = mybir.dt.bfloat16
@@ -11,6 +12,7 @@ U8 = mybir.dt.uint8
 FP8X4 = mybir.dt.float8_e4m3fn_x4
 ALU = mybir.AluOpType
 COPY = mybir.ActivationFunctionType.Copy
+RELU = mybir.ActivationFunctionType.Relu
 
 P = 128
 PACK = 4
@@ -26,8 +28,9 @@ def tile_picked_ccmpclampbtrim_none_po_kernel(
     nc = tc.nc
     with ExitStack() as ctx:
         keep = ctx.enter_context(tc.tile_pool(name="keep", bufs=1))
-        ring = ctx.enter_context(tc.tile_pool(name="ring", bufs=2))
-        psum = ctx.enter_context(tc.psum_pool(name="psum", bufs=8))
+        ring = ctx.enter_context(tc.tile_pool(name="ring", bufs=3))
+        shared = ctx.enter_context(tc.tile_pool(name="shared", bufs=1))
+        psum = ctx.enter_context(tc.psum_pool(name="psum", bufs=1))
 
         def load_list(name, src):
             tile = keep.tile([P, S // 16], U16, name=name)
@@ -36,7 +39,8 @@ def tile_picked_ccmpclampbtrim_none_po_kernel(
 
         def load_scale_rows(tile, src):
             for q in range(4):
-                nc.sync.dma_start(tile[32 * q : 32 * q + 4, :].bitcast(I32), src[0, 4 * q : 4 * q + 4, :].bitcast(I32))
+                rows = src[:, 4 * q : 4 * q + 4, :].bitcast(I32)
+                nc.sync.dma_start(tile[32 * q : 32 * q + 32, :].bitcast(I32), rows.to_broadcast([8, 4, rows.shape[2]]))
 
         def cols(h):
             return slice(h * HALF, (h + 1) * HALF)
@@ -50,9 +54,9 @@ def tile_picked_ccmpclampbtrim_none_po_kernel(
                 src.rearrange("p t (c i) -> p c t i", i=4),
             )
 
-        def product(lhs_w, lhs_s, t, rhs_w, rhs_s, span):
+        def product(lhs_w, lhs_s, t, rhs_w, rhs_s, span, tag, bufs):
             width = span.stop - span.start
-            bank = psum.tile([P, width], F32, name="bank")
+            bank = psum.tile([P, width], F32, name="bank", tag=tag, bufs=bufs)
             m = slice(t * P, (t + 1) * P)
             nc.tensor.matmul_mx(
                 out=bank[:],
@@ -67,10 +71,8 @@ def tile_picked_ccmpclampbtrim_none_po_kernel(
 
         x_s = keep.tile([P, T], U8, name="x_s", align_bytes=64)
         x_w = keep.tile([P, T], U32, name="x_w", align_bytes=64)
-        w_s_raw = keep.tile([P, S], U8, name="w_s_raw", align_bytes=64)
+        w_s_raw = shared.tile([P, S], U8, name="w_s_raw", align_bytes=64, offset=4 * S - S // 2)
         w_w_raw = keep.tile([P, S], U32, name="w_w_raw", align_bytes=64)
-        nc.vector.memset(x_s[:].bitcast(I32), 0)
-        nc.vector.memset(w_s_raw[:].bitcast(I32), 0)
 
         l_offs = load_list("l_offs", offs)
         load_scale_rows(x_s, x_scales)
@@ -91,13 +93,16 @@ def tile_picked_ccmpclampbtrim_none_po_kernel(
         win_a = [keep.tile([P, 2 * S], F32, name=f"win_a{t}") for t in range(PACK)]
         win_b = [keep.tile([P, 2 * S], F32, name=f"win_b{t}") for t in range(PACK)]
         for t in range(PACK):
-            nc.gpsimd.memset(win_a[t][:, S:], 0.0)
+            nc.vector.memset(win_a[t][:, S:].bitcast(I32), 0)
+
+        ident = keep.tile([P, P], F32, name="ident")
+        make_identity(nc, ident[:])
 
         neg_gain = keep.tile([P, PACK], F32, name="neg_gain")
         nc.scalar.activation(neg_gain[:], gain[:], COPY, scale=-1.0)
 
         xq_s = keep.tile([P, S], U8, name="xq_s", align_bytes=64)
-        xq_w = keep.tile([P, S], U32, name="xq_w", align_bytes=64)
+        xq_w = shared.tile([P, S], U32, name="xq_w", align_bytes=64, offset=0)
         nc.vector.tensor_copy(xq_s[:], x_s[:].indirect(l_offs[:]))
         w_w = keep.tile([P, S], U32, name="w_w", align_bytes=64)
         w_s = keep.tile([P, S], U8, name="w_s", align_bytes=64)
@@ -120,34 +125,36 @@ def tile_picked_ccmpclampbtrim_none_po_kernel(
             )
             return dealt
 
-        def pick_words(name, lst, tag):
-            dealt = keep.tile([P, S], U32, name=name, tag=tag, align_bytes=64)
+        def pick_words(dealt, lst):
             nc.vector.tensor_copy(dealt[:].rearrange("p (t m) -> p m t", t=PACK), x_w[:].indirect(lst[:]))
             return dealt
 
         ca_s = pick_scales("ca_s", l_ca, "ca_s_listed")
-        ca_w = pick_words("ca_w", l_ca, "w_s_raw")
+        ca_w = pick_words(shared.tile([P, S], U32, name="ca_w", align_bytes=64, offset=4 * S), l_ca)
 
         spans = [[cols(0), cols(1)]] + [[slice(0, S)]] * (PACK - 1)
         y_banks = []
         for t in range(PACK):
             for span in spans[t]:
-                bank = product(w_w, w_s, t, xq_w, xq_s, span)
+                tag, bufs = ("turned", 1) if span == cols(0) else ("held", PACK)
+                bank = product(w_w, w_s, t, xq_w, xq_s, span, tag, bufs)
                 nc.scalar.copy(win_a[t][:, span], bank[:])
                 nc.scalar.copy(win_b[t][:, S + span.start : S + span.stop], bank[:])
                 y_banks.append((t, span, bank))
 
-        rest = []
+        d2 = [keep.tile([P, S], F32, name=f"d2_{t}") for t in range(PACK)]
+        d3 = [keep.tile([P, S], F32, name=f"d3_{t}") for t in range(PACK)]
+        rest = [keep.tile([P, S], F32, name=f"rest{t}", align_bytes=64) for t in range(PACK)]
+        nc.vector.tensor_tensor(d2[0][:], win_a[0][:].indirect(l_n2[:]), win_b[0][:, S:], ALU.subtract)
         for t in range(PACK):
-            d2 = ring.tile([P, S], F32, name="d2")
-            d3 = ring.tile([P, S], F32, name="d3")
-            nc.vector.tensor_tensor(d2[:], win_a[t][:].indirect(l_n2[:]), win_b[t][:, S:], ALU.subtract)
-            nc.vector.tensor_tensor(d3[:], win_a[t][:].indirect(l_n3[:]), win_b[t][:, S:], ALU.subtract)
+            nc.vector.tensor_tensor(d3[t][:], win_a[t][:].indirect(l_n3[:]), win_b[t][:, S:], ALU.subtract)
+            if t + 1 < PACK:
+                nc.vector.tensor_tensor(
+                    d2[t + 1][:], win_a[t + 1][:].indirect(l_n2[:]), win_b[t + 1][:, S:], ALU.subtract
+                )
             top = ring.tile([P, S], F32, name="top")
-            nc.vector.tensor_tensor(top[:], d2[:], d3[:], ALU.max)
-            r = keep.tile([P, S], F32, name=f"rest{t}", align_bytes=64)
-            nc.scalar.activation(r[:], top[:], COPY, scale=neg_gain[:, t : t + 1])
-            rest.append(r)
+            nc.vector.tensor_tensor(top[:], d2[t][:], d3[t][:], ALU.max)
+            nc.scalar.activation(rest[t][:], top[:], COPY, scale=neg_gain[:, t : t + 1])
             for tt, span, bank in y_banks:
                 if tt == t:
                     nc.scalar.activation(win_b[t][:, span], bank[:], COPY, scale=gain[:, t : t + 1])
@@ -156,35 +163,69 @@ def tile_picked_ccmpclampbtrim_none_po_kernel(
         z_s = keep.tile([P, S], U8, name="z_s", align_bytes=64)
         a_first = []
         for h in range(2):
-            z = keep.tile([P, PACK, HALF], F32, name=f"z{h}")
+            z = keep.tile([P, PACK, HALF], F32, name=f"z{h}", tag=f"d{2 + h}_{PACK - 1}")
             for t in range(PACK):
                 nc.vector.tensor_tensor(z[:, t, :], win_b[t][:].indirect(entries(l_n1, h)), rest[t][:, cols(h)], ALU.add)
             zb = keep.tile([P, PACK * HALF], BF16, name=f"zb{h}", align_bytes=64)
             weave(nc.scalar.copy, zb[:], z[:])
             nc.vector.quantize_mx(out=z_w[:, cols(h)].bitcast(FP8X4), scales=z_s[:, cols(h)], in_=zb[:])
-            a_first.append(product(ca_w, ca_s, 0, z_w, z_s, cols(h)))
+            a_first.append(product(ca_w, ca_s, 0, z_w, z_s, cols(h), "score", 3))
 
-        cb_w = pick_words("cb_w", l_cb, f"rest{PACK - 1}")
+        cb_w = pick_words(keep.tile([P, S], U32, name="cb_w", tag=f"rest{PACK - 1}", align_bytes=64), l_cb)
         cb_s = pick_scales("cb_s", l_cb, "zb1")
 
-        low = []
-        for t in range(PACK):
+        a_plain = [keep.tile([P, S], F32, name=f"a_plain{t}") for t in range(PACK)]
+
+        def score_a(t):
             if t == 0:
                 a_banks = [(cols(h), a_first[h]) for h in range(2)]
             else:
-                a_banks = [(slice(0, S), product(ca_w, ca_s, t, z_w, z_s, slice(0, S)))]
+                a_banks = [(slice(0, S), product(ca_w, ca_s, t, z_w, z_s, slice(0, S), "score", 3))]
             for span, bank in a_banks:
-                nc.scalar.activation(win_a[t][:, span], bank[:], COPY, scale=0.0625)
-                nc.scalar.activation(win_b[t][:, S + span.start : S + span.stop], bank[:], COPY, scale=0.125)
-            bank = product(cb_w, cb_s, t, z_w, z_s, slice(0, S))
+                nc.scalar.activation(win_a[t][:, span], bank[:], COPY, scale=0.03125)
+                nc.scalar.activation(a_plain[t][:, span], bank[:], COPY, scale=0.0625)
+
+        def score_b(t):
+            bank = product(cb_w, cb_s, t, z_w, z_s, slice(0, S), "score", 3)
             nc.scalar.activation(win_b[t][:, :S], bank[:], COPY, scale=0.0625)
-            d4 = ring.tile([P, S], F32, name="d2")
-            g5 = ring.tile([P, S], F32, name="d3")
-            nc.vector.tensor_tensor(d4[:], win_a[t][:].indirect(l_n4[:]), win_b[t][:, S:], ALU.subtract)
-            nc.vector.tensor_copy(g5[:], win_b[t][:].indirect(l_n5[:]))
-            lo = keep.tile([P, S], F32, name=f"low{t}")
-            nc.vector.scalar_tensor_tensor(lo[:], d4[:], -0.5, g5[:], ALU.mult, ALU.min)
-            low.append(lo)
+
+        neg_d = [keep.tile([P, S], F32, name=f"neg_d{t}") for t in range(PACK)]
+
+        def damp(t):
+            nc.vector.tensor_tensor(neg_d[t][:], win_a[t][:].indirect(l_n4[:]), a_plain[t][:], ALU.subtract)
+
+        score_a(0)
+        score_a(1)
+        score_b(0)
+        score_a(2)
+        score_b(1)
+        damp(0)
+        g6_first = keep.tile([P, PACK, HALF], F32, name="g6_first")
+        neg_low = []
+        for t in range(PACK):
+            if t + 1 < PACK:
+                damp(t + 1)
+            gap = keep.tile([P, S], F32, name=f"gap{t}")
+            nc.vector.tensor_tensor(gap[:], win_b[t][:].indirect(l_n5[:]), neg_d[t][:], ALU.add)
+            nc.vector.tensor_copy(g6_first[:, t, :], win_b[t][:].indirect(entries(l_n6, 0)))
+            cut = keep.tile([P, S], F32, name="cut")
+            nc.scalar.activation(cut[:], gap[:], RELU, scale=-1.0)
+            if t + 3 < PACK:
+                score_a(t + 3)
+            turned = psum.tile([P, S], F32, name="turned", tag="turned", bufs=1)
+            for c in range(PACK):
+                blk = slice(c * P, (c + 1) * P)
+                nc.tensor.matmul(turned[:, blk], neg_d[t][:, blk], ident[:], start=True, stop=False, is_transpose=True)
+                nc.tensor.matmul(turned[:, blk], cut[:, blk], ident[:], start=False, stop=True, is_transpose=True)
+            turned_sb = ring.tile([P, S], F32, name="turned_sb")
+            nc.scalar.copy(turned_sb[:], turned[:])
+            if t + 2 < PACK:
+                score_b(t + 2)
+            back = psum.tile([P, S], F32, name="back", tag="held", bufs=PACK)
+            for c in range(PACK):
+                blk = slice(c * P, (c + 1) * P)
+                nc.tensor.transpose(back[:, blk], turned_sb[:, blk], ident[:])
+            neg_low.append(back)
 
         o_w = keep.tile([P, S], U32, name="o_w", align_bytes=64)
         o_s = keep.tile([P, S], U8, name="o_s", align_bytes=64)
@@ -192,10 +233,19 @@ def tile_picked_ccmpclampbtrim_none_po_kernel(
         out_words = out_1[0].rearrange("p c r -> p (c r)").bitcast(I32)
         for h in range(2):
             o = keep.tile([P, PACK, HALF], F32, name=f"o{h}")
-            g6 = keep.tile([P, PACK, HALF], F32, name=f"g6{h}")
-            for t in range(PACK):
-                nc.vector.tensor_copy(g6[:, t, :], win_b[t][:].indirect(entries(l_n6, h)))
-                nc.vector.tensor_tensor(o[:, t, :], low[t][:, cols(h)], g6[:, t, :], ALU.max)
+            for t0 in range(0, PACK, 2):
+                if h == 0:
+                    pair = g6_first[:, t0 : t0 + 2, :]
+                else:
+                    tag = f"gap{PACK - 1}" if t0 == 0 else "g6_first"
+                    pair = keep.tile([P, 2, HALF], F32, name=f"g6_pair{t0}", tag=tag)
+                    for u in range(2):
+                        nc.vector.tensor_copy(pair[:, u, :], win_b[t0 + u][:].indirect(entries(l_n6, h)))
+                for u in range(2):
+                    t = t0 + u
+                    nc.vector.scalar_tensor_tensor(
+                        o[:, t, :], neg_low[t][:, cols(h)], -1.0, pair[:, u, :], ALU.mult, ALU.max
+                    )
             if h == 0:
                 nc.sync.dma_start(out_rows[:, :, cols(h)], o[:])
                 parts = [(nc.scalar.copy, 0, HALF)]

@@ -16,9 +16,14 @@ RELU = mybir.ActivationFunctionType.Relu
 
 P = 128
 PACK = 4
+LAST = PACK - 1
 T = 2048
 S = 512
 HALF = S // 2
+QUARTER = S // 4
+ROW_BYTES = 4 * S
+SUMMED = 2
+HELD, TURNED, QUICK = ("held", 4), ("turned", 2), ("quick", 2)
 FLOPS = 3 * 2 * 512 * 512 * 512
 
 
@@ -29,7 +34,8 @@ def tile_picked_ccmpclampbtrim_none_po_kernel(
     with ExitStack() as ctx:
         keep = ctx.enter_context(tc.tile_pool(name="keep", bufs=1))
         ring = ctx.enter_context(tc.tile_pool(name="ring", bufs=3))
-        shared = ctx.enter_context(tc.tile_pool(name="shared", bufs=1))
+        head = ctx.enter_context(tc.tile_pool(name="head", bufs=1))
+        relay = ctx.enter_context(tc.tile_pool(name="relay", bufs=1))
         psum = ctx.enter_context(tc.psum_pool(name="psum", bufs=1))
 
         def load_list(name, src):
@@ -37,10 +43,12 @@ def tile_picked_ccmpclampbtrim_none_po_kernel(
             nc.sync.dma_start(tile[:], src)
             return tile
 
+        def load_words(tile, src):
+            nc.sync.dma_start(tile[:].bitcast(I32), src[0].rearrange("p n t -> p (n t)").bitcast(I32))
+
         def load_scale_rows(tile, src):
             for q in range(4):
-                rows = src[:, 4 * q : 4 * q + 4, :].bitcast(I32)
-                nc.sync.dma_start(tile[32 * q : 32 * q + 32, :].bitcast(I32), rows.to_broadcast([8, 4, rows.shape[2]]))
+                nc.sync.dma_start(tile[32 * q : 32 * q + 4, :].bitcast(I32), src[0, 4 * q : 4 * q + 4, :].bitcast(I32))
 
         def cols(h):
             return slice(h * HALF, (h + 1) * HALF)
@@ -48,15 +56,22 @@ def tile_picked_ccmpclampbtrim_none_po_kernel(
         def entries(lst, h):
             return lst[:, h * HALF // 16 : (h + 1) * HALF // 16]
 
+        def deal(dst, src):
+            nc.vector.tensor_copy(
+                dst.rearrange("p (t m) -> p t m", t=PACK), src.rearrange("p (m t) -> p t m", t=PACK)
+            )
+
         def weave(engine_copy, dst, src):
             engine_copy(
                 dst.rearrange("p (c i t) -> p c t i", i=4, t=PACK),
                 src.rearrange("p t (c i) -> p c t i", i=4),
             )
 
-        def product(lhs_w, lhs_s, t, rhs_w, rhs_s, span, tag, bufs):
-            width = span.stop - span.start
-            bank = psum.tile([P, width], F32, name="bank", tag=tag, bufs=bufs)
+        def bank_tile(width, kind):
+            return psum.tile([P, width], F32, name="bank", tag=kind[0], bufs=kind[1])
+
+        def product(lhs_w, lhs_s, t, rhs_w, rhs_s, span, kind):
+            bank = bank_tile(span.stop - span.start, kind)
             m = slice(t * P, (t + 1) * P)
             nc.tensor.matmul_mx(
                 out=bank[:],
@@ -69,50 +84,68 @@ def tile_picked_ccmpclampbtrim_none_po_kernel(
             )
             return bank
 
+        def turn(terms):
+            turned = bank_tile(S, TURNED)
+            for c in range(S // P):
+                blk = slice(c * P, (c + 1) * P)
+                for i, term in enumerate(terms):
+                    nc.tensor.matmul(
+                        turned[:, blk],
+                        term[:, blk],
+                        ident[:],
+                        start=(i == 0),
+                        stop=(i == len(terms) - 1),
+                        is_transpose=True,
+                    )
+            return turned
+
+        def turn_back(turned, turned_sb, kind):
+            nc.scalar.copy(turned_sb[:], turned[:])
+            back = bank_tile(S, kind)
+            for c in range(S // P):
+                blk = slice(c * P, (c + 1) * P)
+                nc.tensor.transpose(back[:, blk], turned_sb[:, blk], ident[:])
+            return back
+
         x_s = keep.tile([P, T], U8, name="x_s", align_bytes=64)
         x_w = keep.tile([P, T], U32, name="x_w", align_bytes=64)
-        w_s_raw = shared.tile([P, S], U8, name="w_s_raw", align_bytes=64, offset=4 * S - S // 2)
+        w_s_raw = head.tile([P, S], U8, name="w_s_raw", align_bytes=64, offset=ROW_BYTES - S // 2)
         w_w_raw = keep.tile([P, S], U32, name="w_w_raw", align_bytes=64)
+        nc.gpsimd.memset(x_s[:, : T // 2].bitcast(I32), 0)
+        nc.vector.memset(x_s[:, T // 2 :].bitcast(I32), 0)
+        nc.gpsimd.memset(w_s_raw[:].bitcast(I32), 0)
 
         l_offs = load_list("l_offs", offs)
         load_scale_rows(x_s, x_scales)
+        load_words(w_w_raw, w1_words)
         l_ca = load_list("l_ca", ca)
-        nc.sync.dma_start(w_w_raw[:].bitcast(I32), w1_words[0].rearrange("p n t -> p (n t)").bitcast(I32))
-        nc.sync.dma_start(x_w[:].bitcast(I32), x_words[0].rearrange("p n t -> p (n t)").bitcast(I32))
+        l_n2 = load_list("l_n2", n2)
+        l_n3 = load_list("l_n3", n3)
+        load_words(x_w, x_words)
         load_scale_rows(w_s_raw, w1_scales)
         gain = keep.tile([P, PACK], F32, name="gain")
         nc.sync.dma_start(gain[:], gs.rearrange("(p t) o -> p (t o)", t=PACK))
-        l_n2 = load_list("l_n2", n2)
-        l_n3 = load_list("l_n3", n3)
         l_n1 = load_list("l_n1", n1)
         l_cb = load_list("l_cb", cb)
         l_n4 = load_list("l_n4", n4)
         l_n5 = load_list("l_n5", n5)
         l_n6 = load_list("l_n6", n6)
 
-        win_a = [keep.tile([P, 2 * S], F32, name=f"win_a{t}") for t in range(PACK)]
-        win_b = [keep.tile([P, 2 * S], F32, name=f"win_b{t}") for t in range(PACK)]
-        for t in range(PACK):
-            nc.vector.memset(win_a[t][:, S:].bitcast(I32), 0)
-
         ident = keep.tile([P, P], F32, name="ident")
         make_identity(nc, ident[:])
 
-        neg_gain = keep.tile([P, PACK], F32, name="neg_gain")
-        nc.scalar.activation(neg_gain[:], gain[:], COPY, scale=-1.0)
+        win_a = [keep.tile([P, 2 * S], F32, name=f"win_a{t}") for t in range(PACK)]
+        win_b = [keep.tile([P, 2 * S], F32, name=f"win_b{t}") for t in range(PACK)]
+        for t in range(PACK):
+            (nc.vector if t < PACK // 2 else nc.gpsimd).memset(win_a[t][:, S:], 0.0)
 
         xq_s = keep.tile([P, S], U8, name="xq_s", align_bytes=64)
-        xq_w = shared.tile([P, S], U32, name="xq_w", align_bytes=64, offset=0)
+        xq_w = head.tile([P, S], U32, name="xq_w", align_bytes=64, offset=0)
         nc.vector.tensor_copy(xq_s[:], x_s[:].indirect(l_offs[:]))
         w_w = keep.tile([P, S], U32, name="w_w", align_bytes=64)
         w_s = keep.tile([P, S], U8, name="w_s", align_bytes=64)
-        nc.vector.tensor_copy(
-            w_w[:].bitcast(I32).rearrange("p (t m) -> p t m", t=PACK),
-            w_w_raw[:].bitcast(I32).rearrange("p (m t) -> p t m", t=PACK),
-        )
-        nc.vector.tensor_copy(
-            w_s[:].rearrange("p (t m) -> p t m", t=PACK), w_s_raw[:].rearrange("p (m t) -> p t m", t=PACK)
-        )
+        deal(w_w[:].bitcast(I32), w_w_raw[:].bitcast(I32))
+        deal(w_s[:], w_s_raw[:])
         for h in range(2):
             nc.vector.tensor_copy(xq_w[:, cols(h)], x_w[:].indirect(entries(l_offs, h)))
 
@@ -120,9 +153,7 @@ def tile_picked_ccmpclampbtrim_none_po_kernel(
             listed = keep.tile([P, S], U8, name=name + "_listed", tag=tag, align_bytes=64)
             nc.vector.tensor_copy(listed[:], x_s[:].indirect(lst[:]))
             dealt = keep.tile([P, S], U8, name=name, align_bytes=64)
-            nc.vector.tensor_copy(
-                dealt[:].rearrange("p (t m) -> p t m", t=PACK), listed[:].rearrange("p (m t) -> p t m", t=PACK)
-            )
+            deal(dealt[:], listed[:])
             return dealt
 
         def pick_words(dealt, lst):
@@ -130,135 +161,168 @@ def tile_picked_ccmpclampbtrim_none_po_kernel(
             return dealt
 
         ca_s = pick_scales("ca_s", l_ca, "ca_s_listed")
-        ca_w = pick_words(shared.tile([P, S], U32, name="ca_w", align_bytes=64, offset=4 * S), l_ca)
+        ca_w = pick_words(head.tile([P, S], U32, name="ca_w", align_bytes=64, offset=ROW_BYTES), l_ca)
 
-        spans = [[cols(0), cols(1)]] + [[slice(0, S)]] * (PACK - 1)
-        y_banks = []
-        for t in range(PACK):
-            for span in spans[t]:
-                tag, bufs = ("turned", 1) if span == cols(0) else ("held", PACK)
-                bank = product(w_w, w_s, t, xq_w, xq_s, span, tag, bufs)
-                nc.scalar.copy(win_a[t][:, span], bank[:])
-                nc.scalar.copy(win_b[t][:, S + span.start : S + span.stop], bank[:])
-                y_banks.append((t, span, bank))
+        y_banks = [
+            [
+                (cols(0), product(w_w, w_s, 0, xq_w, xq_s, cols(0), TURNED)),
+                (cols(1), product(w_w, w_s, 0, xq_w, xq_s, cols(1), HELD)),
+            ]
+        ]
+        for t in range(1, PACK):
+            y_banks.append([(slice(0, S), product(w_w, w_s, t, xq_w, xq_s, slice(0, S), HELD))])
 
-        d2 = [keep.tile([P, S], F32, name=f"d2_{t}") for t in range(PACK)]
-        d3 = [keep.tile([P, S], F32, name=f"d3_{t}") for t in range(PACK)]
-        rest = [keep.tile([P, S], F32, name=f"rest{t}", align_bytes=64) for t in range(PACK)]
-        nc.vector.tensor_tensor(d2[0][:], win_a[0][:].indirect(l_n2[:]), win_b[0][:, S:], ALU.subtract)
-        for t in range(PACK):
-            nc.vector.tensor_tensor(d3[t][:], win_a[t][:].indirect(l_n3[:]), win_b[t][:, S:], ALU.subtract)
-            if t + 1 < PACK:
-                nc.vector.tensor_tensor(
-                    d2[t + 1][:], win_a[t + 1][:].indirect(l_n2[:]), win_b[t + 1][:, S:], ALU.subtract
-                )
-            top = ring.tile([P, S], F32, name="top")
-            nc.vector.tensor_tensor(top[:], d2[t][:], d3[t][:], ALU.max)
-            nc.scalar.activation(rest[t][:], top[:], COPY, scale=neg_gain[:, t : t + 1])
-            for tt, span, bank in y_banks:
-                if tt == t:
-                    nc.scalar.activation(win_b[t][:, span], bank[:], COPY, scale=gain[:, t : t + 1])
+        def evict_y(t, dst, scale):
+            for span, bank in y_banks[t]:
+                nc.scalar.activation(dst[:, span], bank[:], COPY, scale=scale)
+
+        def evict_weighted(t):
+            evict_y(t, win_b[t][:, :S], gain[:, t : t + 1])
+
+        by_n2 = [keep.tile([P, S], F32, name=f"by_n2_{t}") for t in range(PACK)]
+        by_n3 = [keep.tile([P, S], F32, name=f"by_n3_{t}", align_bytes=64) for t in range(PACK)]
+        rest = [
+            [keep.tile([P, HALF], F32, name=f"rest{t}_{h}", align_bytes=64) for h in range(2)] for t in range(PACK)
+        ]
+
+        def weigh(t, excess):
+            for h in range(2):
+                nc.scalar.activation(rest[t][h][:], excess[:, cols(h)], COPY, scale=gain[:, t : t + 1])
+
+        def sum_excess(t):
+            nc.scalar.activation(win_b[t][:, S:], by_n3[t][:], RELU, scale=-1.0)
+            return turn([by_n2[t], win_b[t][:, S:], win_a[t][:, :S]])
+
+        for t in range(SUMMED):
+            evict_y(t, win_a[t][:, :S], -1.0)
+        for t in range(SUMMED):
+            nc.vector.tensor_scalar(by_n2[t][:], win_a[t][:].indirect(l_n2[:]), -1.0, 0.0, ALU.mult, ALU.add)
+            nc.vector.tensor_tensor(by_n3[t][:], win_a[t][:].indirect(l_n3[:]), by_n2[t][:], ALU.add)
+        evict_weighted(0)
+        evict_y(2, win_a[2][:, :S], 1.0)
+        evict_y(2, win_b[2][:, S:], 1.0)
+        summed0 = sum_excess(0)
+        evict_weighted(1)
+        evict_y(3, win_a[3][:, :S], 1.0)
+        evict_y(3, win_b[3][:, S:], 1.0)
+        summed1 = sum_excess(1)
+        excess0 = turn_back(summed0, ring.tile([P, S], F32, name="turned_sb"), QUICK)
+        evict_weighted(2)
+        evict_weighted(3)
+        excess1 = turn_back(summed1, relay.tile([P, S], F32, name="turned_late", offset=ROW_BYTES // 2), QUICK)
+        weigh(0, excess0)
+        weigh(1, excess1)
+        for t in range(SUMMED, PACK):
+            nc.vector.tensor_tensor(by_n2[t][:], win_a[t][:].indirect(l_n2[:]), win_b[t][:, S:], ALU.subtract)
+            nc.vector.tensor_tensor(by_n3[t][:], win_a[t][:].indirect(l_n3[:]), win_b[t][:, S:], ALU.subtract)
+        for t in range(SUMMED, PACK):
+            excess = relay.tile([P, S], F32, name=f"excess{t}", offset=(t - SUMMED) * ROW_BYTES)
+            nc.vector.tensor_tensor(excess[:], by_n2[t][:], by_n3[t][:], ALU.max)
+            weigh(t, excess)
 
         z_w = keep.tile([P, S], U32, name="z_w", align_bytes=64)
         z_s = keep.tile([P, S], U8, name="z_s", align_bytes=64)
-        a_first = []
-        for h in range(2):
-            z = keep.tile([P, PACK, HALF], F32, name=f"z{h}", tag=f"d{2 + h}_{PACK - 1}")
+        a0_banks = []
+        for h, tag in enumerate((f"by_n3_{LAST}", f"rest{LAST}_0")):
+            z = keep.tile([P, PACK, HALF], F32, name=f"z{h}", tag=tag, align_bytes=64)
             for t in range(PACK):
-                nc.vector.tensor_tensor(z[:, t, :], win_b[t][:].indirect(entries(l_n1, h)), rest[t][:, cols(h)], ALU.add)
-            zb = keep.tile([P, PACK * HALF], BF16, name=f"zb{h}", align_bytes=64)
-            weave(nc.scalar.copy, zb[:], z[:])
-            nc.vector.quantize_mx(out=z_w[:, cols(h)].bitcast(FP8X4), scales=z_s[:, cols(h)], in_=zb[:])
-            a_first.append(product(ca_w, ca_s, 0, z_w, z_s, cols(h), "score", 3))
+                nc.vector.tensor_tensor(z[:, t, :], win_b[t][:].indirect(entries(l_n1, h)), rest[t][h][:], ALU.subtract)
+            z_bf = keep.tile([P, PACK * HALF], BF16, name=f"z_bf{h}", align_bytes=64)
+            weave(nc.scalar.copy, z_bf[:], z[:])
+            nc.vector.quantize_mx(out=z_w[:, cols(h)].bitcast(FP8X4), scales=z_s[:, cols(h)], in_=z_bf[:])
+            a0_banks.append((cols(h), product(ca_w, ca_s, 0, z_w, z_s, cols(h), QUICK)))
 
-        cb_w = pick_words(keep.tile([P, S], U32, name="cb_w", tag=f"rest{PACK - 1}", align_bytes=64), l_cb)
-        cb_s = pick_scales("cb_s", l_cb, "zb1")
+        cb_w = pick_words(keep.tile([P, S], U32, name="cb_w", tag=f"rest{LAST}_1", align_bytes=64), l_cb)
+        cb_s = pick_scales("cb_s", l_cb, "z_bf1")
 
         a_plain = [keep.tile([P, S], F32, name=f"a_plain{t}") for t in range(PACK)]
-
-        def score_a(t):
-            if t == 0:
-                a_banks = [(cols(h), a_first[h]) for h in range(2)]
-            else:
-                a_banks = [(slice(0, S), product(ca_w, ca_s, t, z_w, z_s, slice(0, S), "score", 3))]
-            for span, bank in a_banks:
-                nc.scalar.activation(win_a[t][:, span], bank[:], COPY, scale=0.03125)
-                nc.scalar.activation(a_plain[t][:, span], bank[:], COPY, scale=0.0625)
-
-        def score_b(t):
-            bank = product(cb_w, cb_s, t, z_w, z_s, slice(0, S), "score", 3)
-            nc.scalar.activation(win_b[t][:, :S], bank[:], COPY, scale=0.0625)
-
         neg_d = [keep.tile([P, S], F32, name=f"neg_d{t}") for t in range(PACK)]
+        gap = [keep.tile([P, S], F32, name=f"gap{t}") for t in range(PACK)]
 
-        def damp(t):
+        def make_a(t):
+            whole = slice(0, S)
+            for span, bank in a0_banks if t == 0 else [(whole, product(ca_w, ca_s, t, z_w, z_s, whole, QUICK))]:
+                nc.scalar.activation(win_a[t][:, span], bank[:], COPY, scale=1 / 32)
+                nc.scalar.activation(a_plain[t][:, span], bank[:], COPY, scale=1 / 16)
+
+        def make_b(t):
+            bank = product(cb_w, cb_s, t, z_w, z_s, slice(0, S), HELD)
+            nc.scalar.activation(win_b[t][:, :S], bank[:], COPY, scale=1 / 16)
+
+        def fetch_n4(t):
             nc.vector.tensor_tensor(neg_d[t][:], win_a[t][:].indirect(l_n4[:]), a_plain[t][:], ALU.subtract)
 
-        score_a(0)
-        score_a(1)
-        score_b(0)
-        score_a(2)
-        score_b(1)
-        damp(0)
-        g6_first = keep.tile([P, PACK, HALF], F32, name="g6_first")
+        def fetch_n5(t):
+            nc.vector.tensor_tensor(gap[t][:], win_b[t][:].indirect(l_n5[:]), neg_d[t][:], ALU.add)
+
+        def sum_neg_low(t):
+            cut = keep.tile([P, S], F32, name="cut", bufs=2)
+            nc.scalar.activation(cut[:], gap[t][:], RELU, scale=-1.0)
+            return turn([neg_d[t], cut])
+
+        make_a(0)
+        make_a(1)
+        make_b(0)
+        make_a(2)
+        make_b(1)
+        make_b(2)
+        fetch_n4(0)
+        fetch_n4(1)
+        fetch_n5(0)
+        fetch_n4(2)
+        fetch_n5(1)
+        fetch_n5(2)
+        summed = [sum_neg_low(0)]
+        make_b(LAST)
+        make_a(LAST)
+        fetch_n4(LAST)
+        fetch_n5(LAST)
         neg_low = []
         for t in range(PACK):
-            if t + 1 < PACK:
-                damp(t + 1)
-            gap = keep.tile([P, S], F32, name=f"gap{t}")
-            nc.vector.tensor_tensor(gap[:], win_b[t][:].indirect(l_n5[:]), neg_d[t][:], ALU.add)
-            nc.vector.tensor_copy(g6_first[:, t, :], win_b[t][:].indirect(entries(l_n6, 0)))
-            cut = keep.tile([P, S], F32, name="cut")
-            nc.scalar.activation(cut[:], gap[:], RELU, scale=-1.0)
-            if t + 3 < PACK:
-                score_a(t + 3)
-            turned = psum.tile([P, S], F32, name="turned", tag="turned", bufs=1)
-            for c in range(PACK):
-                blk = slice(c * P, (c + 1) * P)
-                nc.tensor.matmul(turned[:, blk], neg_d[t][:, blk], ident[:], start=True, stop=False, is_transpose=True)
-                nc.tensor.matmul(turned[:, blk], cut[:, blk], ident[:], start=False, stop=True, is_transpose=True)
-            turned_sb = ring.tile([P, S], F32, name="turned_sb")
-            nc.scalar.copy(turned_sb[:], turned[:])
-            if t + 2 < PACK:
-                score_b(t + 2)
-            back = psum.tile([P, S], F32, name="back", tag="held", bufs=PACK)
-            for c in range(PACK):
-                blk = slice(c * P, (c + 1) * P)
-                nc.tensor.transpose(back[:, blk], turned_sb[:, blk], ident[:])
-            neg_low.append(back)
+            if t < LAST:
+                summed.append(sum_neg_low(t + 1))
+            neg_low.append(turn_back(summed[t], ring.tile([P, S], F32, name="turned_sb"), HELD))
 
         o_w = keep.tile([P, S], U32, name="o_w", align_bytes=64)
         o_s = keep.tile([P, S], U8, name="o_s", align_bytes=64)
         out_rows = out_0.rearrange("(p t) j -> p t j", t=PACK)
         out_words = out_1[0].rearrange("p c r -> p (c r)").bitcast(I32)
-        for h in range(2):
-            o = keep.tile([P, PACK, HALF], F32, name=f"o{h}")
-            for t0 in range(0, PACK, 2):
-                if h == 0:
-                    pair = g6_first[:, t0 : t0 + 2, :]
-                else:
-                    tag = f"gap{PACK - 1}" if t0 == 0 else "g6_first"
-                    pair = keep.tile([P, 2, HALF], F32, name=f"g6_pair{t0}", tag=tag)
-                    for u in range(2):
-                        nc.vector.tensor_copy(pair[:, u, :], win_b[t0 + u][:].indirect(entries(l_n6, h)))
-                for u in range(2):
-                    t = t0 + u
-                    nc.vector.scalar_tensor_tensor(
-                        o[:, t, :], neg_low[t][:, cols(h)], -1.0, pair[:, u, :], ALU.mult, ALU.max
-                    )
-            if h == 0:
-                nc.sync.dma_start(out_rows[:, :, cols(h)], o[:])
-                parts = [(nc.scalar.copy, 0, HALF)]
-            else:
-                nc.sync.dma_start(out_rows[:, 0:2, cols(h)], o[:, 0:2, :])
-                nc.sync.dma_start(out_rows[:, 2:4, cols(h)], o[:, 2:4, :])
-                parts = [(nc.vector.tensor_copy, 0, HALF // 2), (nc.scalar.copy, HALF // 2, HALF)]
-            for copy, c0, c1 in parts:
-                ob = keep.tile([P, PACK * (c1 - c0)], BF16, name=f"ob{h}_{c0}", align_bytes=64)
-                weave(copy, ob[:], o[:, :, c0:c1])
-                span = slice(h * HALF + c0, h * HALF + c1)
-                nc.vector.quantize_mx(out=o_w[:, span].bitcast(FP8X4), scales=o_s[:, span], in_=ob[:])
-            nc.sync.dma_start(out_words[:, cols(h)], o_w[:, cols(h)].bitcast(I32))
+
+        def fetch_n6(dst, t, h):
+            nc.vector.tensor_copy(dst, win_b[t][:].indirect(entries(l_n6, h)))
+
+        def finish(o, t, h, by_n6, c0, c1):
+            low = neg_low[t][:, h * HALF + c0 : h * HALF + c1]
+            nc.vector.scalar_tensor_tensor(o[:, t, c0:c1], low, -1.0, by_n6[:, c0:c1], ALU.mult, ALU.max)
+
+        def quantise(o, h, engine_copy, c0, c1):
+            o_bf = keep.tile([P, PACK * (c1 - c0)], BF16, name=f"o_bf{h}_{c0}", align_bytes=64)
+            weave(engine_copy, o_bf[:], o[:, :, c0:c1])
+            span = slice(h * HALF + c0, h * HALF + c1)
+            nc.vector.quantize_mx(out=o_w[:, span].bitcast(FP8X4), scales=o_s[:, span], in_=o_bf[:])
+
+        first = keep.tile([P, PACK, HALF], F32, name="by_n6_first", tag=f"a_plain{LAST}")
+        for t in range(PACK):
+            fetch_n6(first[:, t, :], t, 0)
+        o0 = keep.tile([P, PACK, HALF], F32, name="o0")
+        for t in range(PACK):
+            finish(o0, t, 0, first[:, t, :], 0, HALF)
+        nc.sync.dma_start(out_rows[:, :, cols(0)], o0[:])
+        quantise(o0, 0, nc.scalar.copy, 0, HALF)
+        nc.sync.dma_start(out_words[:, cols(0)], o_w[:, cols(0)].bitcast(I32))
+
+        o1 = keep.tile([P, PACK, HALF], F32, name="o1")
+        for t0, tag in ((0, f"gap{LAST}"), (2, f"a_plain{LAST}")):
+            pair = keep.tile([P, 2, HALF], F32, name=f"by_n6_pair{t0}", tag=tag)
+            for u in range(2):
+                fetch_n6(pair[:, u, :], t0 + u, 1)
+            for u in range(2):
+                for c0, c1 in ((QUARTER, HALF), (0, QUARTER)) if t0 + u == LAST else ((0, HALF),):
+                    finish(o1, t0 + u, 1, pair[:, u, :], c0, c1)
+            nc.sync.dma_start(out_rows[:, t0 : t0 + 2, cols(1)], o1[:, t0 : t0 + 2, :])
+        quantise(o1, 1, nc.vector.tensor_copy, 0, QUARTER)
+        quantise(o1, 1, nc.scalar.copy, QUARTER, HALF)
+        nc.sync.dma_start(out_words[:, cols(1)], o_w[:, cols(1)].bitcast(I32))
         for q in range(4):
-            eng = nc.scalar if q % 2 == 0 else nc.sync
-            eng.dma_start(out_2[0, 4 * q : 4 * q + 4, :].bitcast(I32), o_s[32 * q : 32 * q + 4, :].bitcast(I32))
+            queue = nc.scalar if q % 2 == 0 else nc.sync
+            queue.dma_start(out_2[0, 4 * q : 4 * q + 4, :].bitcast(I32), o_s[32 * q : 32 * q + 4, :].bitcast(I32))

from contextlib import ExitStack

import concourse.mybir as mybir
from concourse.masks import make_identity

F32 = mybir.dt.float32
BF16 = mybir.dt.bfloat16
I32 = mybir.dt.int32
U32 = mybir.dt.uint32
U16 = mybir.dt.uint16
U8 = mybir.dt.uint8
FP8X4 = mybir.dt.float8_e4m3fn_x4
ALU = mybir.AluOpType
COPY = mybir.ActivationFunctionType.Copy
RELU = mybir.ActivationFunctionType.Relu

P = 128
PACK = 4
LAST = PACK - 1
T = 2048
S = 512
HALF = S // 2
QUARTER = S // 4
ROW_BYTES = 4 * S
SUMMED = 2
HELD, TURNED, QUICK = ("held", 4), ("turned", 2), ("quick", 2)
FLOPS = 3 * 2 * 512 * 512 * 512


def tile_picked_ccmpclampbtrim_none_po_kernel(
    tc, x_words, x_scales, w1_words, w1_scales, gs, offs, n1, n2, n3, ca, cb, n4, n5, n6, out_0, out_1, out_2
):
    nc = tc.nc
    with ExitStack() as ctx:
        keep = ctx.enter_context(tc.tile_pool(name="keep", bufs=1))
        ring = ctx.enter_context(tc.tile_pool(name="ring", bufs=3))
        head = ctx.enter_context(tc.tile_pool(name="head", bufs=1))
        relay = ctx.enter_context(tc.tile_pool(name="relay", bufs=1))
        psum = ctx.enter_context(tc.psum_pool(name="psum", bufs=1))

        def load_list(name, src):
            tile = keep.tile([P, S // 16], U16, name=name)
            nc.sync.dma_start(tile[:], src)
            return tile

        def load_words(tile, src):
            nc.sync.dma_start(tile[:].bitcast(I32), src[0].rearrange("p n t -> p (n t)").bitcast(I32))

        def load_scale_rows(tile, src):
            for q in range(4):
                nc.sync.dma_start(tile[32 * q : 32 * q + 4, :].bitcast(I32), src[0, 4 * q : 4 * q + 4, :].bitcast(I32))

        def cols(h):
            return slice(h * HALF, (h + 1) * HALF)

        def entries(lst, h):
            return lst[:, h * HALF // 16 : (h + 1) * HALF // 16]

        def deal(dst, src):
            nc.vector.tensor_copy(
                dst.rearrange("p (t m) -> p t m", t=PACK), src.rearrange("p (m t) -> p t m", t=PACK)
            )

        def weave(engine_copy, dst, src):
            engine_copy(
                dst.rearrange("p (c i t) -> p c t i", i=4, t=PACK),
                src.rearrange("p t (c i) -> p c t i", i=4),
            )

        def bank_tile(width, kind):
            return psum.tile([P, width], F32, name="bank", tag=kind[0], bufs=kind[1])

        def product(lhs_w, lhs_s, t, rhs_w, rhs_s, span, kind):
            bank = bank_tile(span.stop - span.start, kind)
            m = slice(t * P, (t + 1) * P)
            nc.tensor.matmul_mx(
                out=bank[:],
                lhsT=lhs_w[:, m].bitcast(FP8X4),
                lhsT_scale=lhs_s[:, m],
                rhs=rhs_w[:, span].bitcast(FP8X4),
                rhs_scale=rhs_s[:, span],
                start=True,
                stop=True,
            )
            return bank

        def turn(terms):
            turned = bank_tile(S, TURNED)
            for c in range(S // P):
                blk = slice(c * P, (c + 1) * P)
                for i, term in enumerate(terms):
                    nc.tensor.matmul(
                        turned[:, blk],
                        term[:, blk],
                        ident[:],
                        start=(i == 0),
                        stop=(i == len(terms) - 1),
                        is_transpose=True,
                    )
            return turned

        def turn_back(turned, turned_sb, kind):
            nc.scalar.copy(turned_sb[:], turned[:])
            back = bank_tile(S, kind)
            for c in range(S // P):
                blk = slice(c * P, (c + 1) * P)
                nc.tensor.transpose(back[:, blk], turned_sb[:, blk], ident[:])
            return back

        x_s = keep.tile([P, T], U8, name="x_s", align_bytes=64)
        x_w = keep.tile([P, T], U32, name="x_w", align_bytes=64)
        w_s_raw = head.tile([P, S], U8, name="w_s_raw", align_bytes=64, offset=ROW_BYTES - S // 2)
        w_w_raw = keep.tile([P, S], U32, name="w_w_raw", align_bytes=64)
        nc.gpsimd.memset(x_s[:, : T // 2].bitcast(I32), 0)
        nc.vector.memset(x_s[:, T // 2 :].bitcast(I32), 0)
        nc.gpsimd.memset(w_s_raw[:].bitcast(I32), 0)

        l_offs = load_list("l_offs", offs)
        load_scale_rows(x_s, x_scales)
        load_words(w_w_raw, w1_words)
        l_ca = load_list("l_ca", ca)
        l_n2 = load_list("l_n2", n2)
        l_n3 = load_list("l_n3", n3)
        load_words(x_w, x_words)
        load_scale_rows(w_s_raw, w1_scales)
        gain = keep.tile([P, PACK], F32, name="gain")
        nc.sync.dma_start(gain[:], gs.rearrange("(p t) o -> p (t o)", t=PACK))
        l_n1 = load_list("l_n1", n1)
        l_cb = load_list("l_cb", cb)
        l_n4 = load_list("l_n4", n4)
        l_n5 = load_list("l_n5", n5)
        l_n6 = load_list("l_n6", n6)

        ident = keep.tile([P, P], F32, name="ident")
        make_identity(nc, ident[:])

        win_a = [keep.tile([P, 2 * S], F32, name=f"win_a{t}") for t in range(PACK)]
        win_b = [keep.tile([P, 2 * S], F32, name=f"win_b{t}") for t in range(PACK)]
        for t in range(PACK):
            (nc.vector if t < PACK // 2 else nc.gpsimd).memset(win_a[t][:, S:], 0.0)

        xq_s = keep.tile([P, S], U8, name="xq_s", align_bytes=64)
        xq_w = head.tile([P, S], U32, name="xq_w", align_bytes=64, offset=0)
        nc.vector.tensor_copy(xq_s[:], x_s[:].indirect(l_offs[:]))
        w_w = keep.tile([P, S], U32, name="w_w", align_bytes=64)
        w_s = keep.tile([P, S], U8, name="w_s", align_bytes=64)
        deal(w_w[:].bitcast(I32), w_w_raw[:].bitcast(I32))
        deal(w_s[:], w_s_raw[:])
        for h in range(2):
            nc.vector.tensor_copy(xq_w[:, cols(h)], x_w[:].indirect(entries(l_offs, h)))

        def pick_scales(name, lst, tag):
            listed = keep.tile([P, S], U8, name=name + "_listed", tag=tag, align_bytes=64)
            nc.vector.tensor_copy(listed[:], x_s[:].indirect(lst[:]))
            dealt = keep.tile([P, S], U8, name=name, align_bytes=64)
            deal(dealt[:], listed[:])
            return dealt

        def pick_words(dealt, lst):
            nc.vector.tensor_copy(dealt[:].rearrange("p (t m) -> p m t", t=PACK), x_w[:].indirect(lst[:]))
            return dealt

        ca_s = pick_scales("ca_s", l_ca, "ca_s_listed")
        ca_w = pick_words(head.tile([P, S], U32, name="ca_w", align_bytes=64, offset=ROW_BYTES), l_ca)

        y_banks = [
            [
                (cols(0), product(w_w, w_s, 0, xq_w, xq_s, cols(0), TURNED)),
                (cols(1), product(w_w, w_s, 0, xq_w, xq_s, cols(1), HELD)),
            ]
        ]
        for t in range(1, PACK):
            y_banks.append([(slice(0, S), product(w_w, w_s, t, xq_w, xq_s, slice(0, S), HELD))])

        def evict_y(t, dst, scale):
            for span, bank in y_banks[t]:
                nc.scalar.activation(dst[:, span], bank[:], COPY, scale=scale)

        def evict_weighted(t):
            evict_y(t, win_b[t][:, :S], gain[:, t : t + 1])

        by_n2 = [keep.tile([P, S], F32, name=f"by_n2_{t}") for t in range(PACK)]
        by_n3 = [keep.tile([P, S], F32, name=f"by_n3_{t}", align_bytes=64) for t in range(PACK)]
        rest = [
            [keep.tile([P, HALF], F32, name=f"rest{t}_{h}", align_bytes=64) for h in range(2)] for t in range(PACK)
        ]

        def weigh(t, excess):
            for h in range(2):
                nc.scalar.activation(rest[t][h][:], excess[:, cols(h)], COPY, scale=gain[:, t : t + 1])

        def sum_excess(t):
            nc.scalar.activation(win_b[t][:, S:], by_n3[t][:], RELU, scale=-1.0)
            return turn([by_n2[t], win_b[t][:, S:], win_a[t][:, :S]])

        for t in range(SUMMED):
            evict_y(t, win_a[t][:, :S], -1.0)
        for t in range(SUMMED):
            nc.vector.tensor_scalar(by_n2[t][:], win_a[t][:].indirect(l_n2[:]), -1.0, 0.0, ALU.mult, ALU.add)
            nc.vector.tensor_tensor(by_n3[t][:], win_a[t][:].indirect(l_n3[:]), by_n2[t][:], ALU.add)
        evict_weighted(0)
        evict_y(2, win_a[2][:, :S], 1.0)
        evict_y(2, win_b[2][:, S:], 1.0)
        summed0 = sum_excess(0)
        evict_weighted(1)
        evict_y(3, win_a[3][:, :S], 1.0)
        evict_y(3, win_b[3][:, S:], 1.0)
        summed1 = sum_excess(1)
        excess0 = turn_back(summed0, ring.tile([P, S], F32, name="turned_sb"), QUICK)
        evict_weighted(2)
        evict_weighted(3)
        excess1 = turn_back(summed1, relay.tile([P, S], F32, name="turned_late", offset=ROW_BYTES // 2), QUICK)
        weigh(0, excess0)
        weigh(1, excess1)
        for t in range(SUMMED, PACK):
            nc.vector.tensor_tensor(by_n2[t][:], win_a[t][:].indirect(l_n2[:]), win_b[t][:, S:], ALU.subtract)
            nc.vector.tensor_tensor(by_n3[t][:], win_a[t][:].indirect(l_n3[:]), win_b[t][:, S:], ALU.subtract)
        for t in range(SUMMED, PACK):
            excess = relay.tile([P, S], F32, name=f"excess{t}", offset=(t - SUMMED) * ROW_BYTES)
            nc.vector.tensor_tensor(excess[:], by_n2[t][:], by_n3[t][:], ALU.max)
            weigh(t, excess)

        z_w = keep.tile([P, S], U32, name="z_w", align_bytes=64)
        z_s = keep.tile([P, S], U8, name="z_s", align_bytes=64)
        a0_banks = []
        for h, tag in enumerate((f"by_n3_{LAST}", f"rest{LAST}_0")):
            z = keep.tile([P, PACK, HALF], F32, name=f"z{h}", tag=tag, align_bytes=64)
            for t in range(PACK):
                nc.vector.tensor_tensor(z[:, t, :], win_b[t][:].indirect(entries(l_n1, h)), rest[t][h][:], ALU.subtract)
            z_bf = keep.tile([P, PACK * HALF], BF16, name=f"z_bf{h}", align_bytes=64)
            weave(nc.scalar.copy, z_bf[:], z[:])
            nc.vector.quantize_mx(out=z_w[:, cols(h)].bitcast(FP8X4), scales=z_s[:, cols(h)], in_=z_bf[:])
            a0_banks.append((cols(h), product(ca_w, ca_s, 0, z_w, z_s, cols(h), QUICK)))

        cb_w = pick_words(keep.tile([P, S], U32, name="cb_w", tag=f"rest{LAST}_1", align_bytes=64), l_cb)
        cb_s = pick_scales("cb_s", l_cb, "z_bf1")

        a_plain = [keep.tile([P, S], F32, name=f"a_plain{t}") for t in range(PACK)]
        neg_d = [keep.tile([P, S], F32, name=f"neg_d{t}") for t in range(PACK)]
        gap = [keep.tile([P, S], F32, name=f"gap{t}") for t in range(PACK)]

        def make_a(t):
            whole = slice(0, S)
            for span, bank in a0_banks if t == 0 else [(whole, product(ca_w, ca_s, t, z_w, z_s, whole, QUICK))]:
                nc.scalar.activation(win_a[t][:, span], bank[:], COPY, scale=1 / 32)
                nc.scalar.activation(a_plain[t][:, span], bank[:], COPY, scale=1 / 16)

        def make_b(t):
            bank = product(cb_w, cb_s, t, z_w, z_s, slice(0, S), HELD)
            nc.scalar.activation(win_b[t][:, :S], bank[:], COPY, scale=1 / 16)

        def fetch_n4(t):
            nc.vector.tensor_tensor(neg_d[t][:], win_a[t][:].indirect(l_n4[:]), a_plain[t][:], ALU.subtract)

        def fetch_n5(t):
            nc.vector.tensor_tensor(gap[t][:], win_b[t][:].indirect(l_n5[:]), neg_d[t][:], ALU.add)

        def sum_neg_low(t):
            cut = keep.tile([P, S], F32, name="cut", bufs=2)
            nc.scalar.activation(cut[:], gap[t][:], RELU, scale=-1.0)
            return turn([neg_d[t], cut])

        make_a(0)
        make_a(1)
        make_b(0)
        make_a(2)
        make_b(1)
        make_b(2)
        fetch_n4(0)
        fetch_n4(1)
        fetch_n5(0)
        fetch_n4(2)
        fetch_n5(1)
        fetch_n5(2)
        summed = [sum_neg_low(0)]
        make_b(LAST)
        make_a(LAST)
        fetch_n4(LAST)
        fetch_n5(LAST)
        neg_low = []
        for t in range(PACK):
            if t < LAST:
                summed.append(sum_neg_low(t + 1))
            neg_low.append(turn_back(summed[t], ring.tile([P, S], F32, name="turned_sb"), HELD))

        o_w = keep.tile([P, S], U32, name="o_w", align_bytes=64)
        o_s = keep.tile([P, S], U8, name="o_s", align_bytes=64)
        out_rows = out_0.rearrange("(p t) j -> p t j", t=PACK)
        out_words = out_1[0].rearrange("p c r -> p (c r)").bitcast(I32)

        def fetch_n6(dst, t, h):
            nc.vector.tensor_copy(dst, win_b[t][:].indirect(entries(l_n6, h)))

        def finish(o, t, h, by_n6, c0, c1):
            low = neg_low[t][:, h * HALF + c0 : h * HALF + c1]
            nc.vector.scalar_tensor_tensor(o[:, t, c0:c1], low, -1.0, by_n6[:, c0:c1], ALU.mult, ALU.max)

        def quantise(o, h, engine_copy, c0, c1):
            o_bf = keep.tile([P, PACK * (c1 - c0)], BF16, name=f"o_bf{h}_{c0}", align_bytes=64)
            weave(engine_copy, o_bf[:], o[:, :, c0:c1])
            span = slice(h * HALF + c0, h * HALF + c1)
            nc.vector.quantize_mx(out=o_w[:, span].bitcast(FP8X4), scales=o_s[:, span], in_=o_bf[:])

        first = keep.tile([P, PACK, HALF], F32, name="by_n6_first", tag=f"a_plain{LAST}")
        for t in range(PACK):
            fetch_n6(first[:, t, :], t, 0)
        o0 = keep.tile([P, PACK, HALF], F32, name="o0")
        for t in range(PACK):
            finish(o0, t, 0, first[:, t, :], 0, HALF)
        nc.sync.dma_start(out_rows[:, :, cols(0)], o0[:])
        quantise(o0, 0, nc.scalar.copy, 0, HALF)
        nc.sync.dma_start(out_words[:, cols(0)], o_w[:, cols(0)].bitcast(I32))

        o1 = keep.tile([P, PACK, HALF], F32, name="o1")
        for t0, tag in ((0, f"gap{LAST}"), (2, f"a_plain{LAST}")):
            pair = keep.tile([P, 2, HALF], F32, name=f"by_n6_pair{t0}", tag=tag)
            for u in range(2):
                fetch_n6(pair[:, u, :], t0 + u, 1)
            for u in range(2):
                for c0, c1 in ((QUARTER, HALF), (0, QUARTER)) if t0 + u == LAST else ((0, HALF),):
                    finish(o1, t0 + u, 1, pair[:, u, :], c0, c1)
            nc.sync.dma_start(out_rows[:, t0 : t0 + 2, cols(1)], o1[:, t0 : t0 + 2, :])
        quantise(o1, 1, nc.vector.tensor_copy, 0, QUARTER)
        quantise(o1, 1, nc.scalar.copy, QUARTER, HALF)
        nc.sync.dma_start(out_words[:, cols(1)], o_w[:, cols(1)].bitcast(I32))
        for q in range(4):
            queue = nc.scalar if q % 2 == 0 else nc.sync
            queue.dma_start(out_2[0, 4 * q : 4 * q + 4, :].bitcast(I32), o_s[32 * q : 32 * q + 4, :].bitcast(I32))
